import numpy as np
import ml_dtypes


def mxq(x, axis, fmt="e4m3"):
    dtype, down = {"e4m3": (ml_dtypes.float8_e4m3fn, 7), "e5m2": (ml_dtypes.float8_e5m2, 14)}[fmt]
    v = np.moveaxis(np.asarray(x, np.float32).astype(ml_dtypes.bfloat16).astype(np.float64), axis, -1)
    blocks = v.reshape(v.shape[:-1] + (-1, 32))
    amax = np.abs(blocks).max(-1, keepdims=True)
    byte = np.maximum(np.where(amax > 0, np.frexp(amax)[1] - 1 + 127, 0) - down, 1)
    scale = np.exp2(byte - 127.0)
    codes = (blocks / scale).astype(np.float32).astype(dtype).astype(np.float64)
    return np.moveaxis((codes * scale).reshape(v.shape), -1, axis)


WIDE = False


def mx_kscale(k):
    if not WIDE:
        return np.ones(k)
    levels = np.array([30, -30])
    if k % 512:
        return np.exp2(np.random.permutation(np.resize(levels, k // 32))).repeat(32)
    a = np.empty((k // 512, 16))
    for p in range(k // 512):
        a[p, :8] = np.random.permutation(np.resize(levels, 8))
        for g in range(8):
            far = levels[np.abs(levels - a[p, g]) >= 10]
            a[p, g + 8] = far[np.random.randint(len(far))]
    return np.exp2(a.ravel()).repeat(32)


def f64(x):
    return np.asarray(x).astype(np.float64)


def striped(idx):
    return np.tile(np.asarray(idx).reshape(-1, 16).T, (8, 1)).astype(np.uint16)


def unstriped(offs):
    return offs[:16].T.reshape(-1).astype(np.int64)


E2M1 = np.array([0.0, 0.5, 1.0, 1.5, 2.0, 3.0, 4.0, 6.0, -0.0, -0.5, -1.0, -1.5, -2.0, -3.0, -4.0, -6.0])


def pack_weight(w, fmt):
    k, n = w.shape
    w = f64(np.asarray(w, np.float32).astype(ml_dtypes.bfloat16)).reshape(k // 32, 32, n)
    amax = np.abs(w).max(1)
    if fmt in ("e4m3", "e5m2"):
        byte = np.frexp(amax)[1] - 1 + 127 - (7 if fmt == "e4m3" else 14)
    else:
        mant, ex = np.frexp(amax / 6.0)
        byte = np.where(mant > 0.5, ex, ex - 1) + 127
    byte = np.clip(np.where(amax > 0, byte, 1), 1, 254)
    scaled = (w * np.exp2(127.0 - byte)[:, None, :]).reshape(k, n).astype(np.float32)
    by_word = np.ascontiguousarray(scaled.reshape(k // 512, 128, 4, n).transpose(0, 1, 3, 2))
    if fmt in ("e4m3", "e5m2"):
        words = by_word.astype(ml_dtypes.float8_e4m3fn if fmt == "e4m3" else ml_dtypes.float8_e5m2).view(np.uint8)
    else:
        c = by_word.astype(ml_dtypes.float4_e2m1fn).view(np.uint8) & 0xF
        words = (c[..., 0::2] | (c[..., 1::2] << 4)).reshape(k // 512, 128, 2 * n)
    return np.ascontiguousarray(words), np.ascontiguousarray(byte.astype(np.uint8).reshape(k // 512, 16, n))


def unpack_weight(words, scales, fmt):
    g, _, n = scales.shape
    words = np.ascontiguousarray(words).reshape(g, 128, n, -1)
    if fmt in ("e4m3", "e5m2"):
        vals = words.view(ml_dtypes.float8_e4m3fn if fmt == "e4m3" else ml_dtypes.float8_e5m2).astype(np.float64)
    else:
        nib = np.empty((g, 128, n, 4), np.uint8)
        nib[..., 0::2] = words & 0xF
        nib[..., 1::2] = words >> 4
        vals = E2M1[nib]
    vals = vals * np.repeat(np.exp2(scales.astype(np.float64) - 127.0), 8, axis=1)[..., None]
    return vals.transpose(0, 1, 3, 2).reshape(g * 512, n)


def sigmoid(v):
    return 1.0 / (1.0 + np.exp(-v))


K, T, J, R, C, O, N, L, E = 512, 2048, 256, 512, 512, 256, 256, 512, 1024


def setup_inputs():
    n = np.random.standard_normal
    idx = np.random.permutation(T)[:J]
    idx2 = np.random.permutation(T)[:J]
    idx3 = np.random.permutation(C)[:J]
    idx4 = np.random.permutation(C)[:J]
    idx5 = np.random.permutation(C)[:O]
    idx6 = np.random.permutation(C)[:O]
    idx7 = np.random.permutation(E)[:O]
    fk = mx_kscale(K)
    fr = mx_kscale(R)
    fl = mx_kscale(L)
    xtp = pack_weight(n((K, T)) / fk[:, None], "e2m1")
    wp = pack_weight(n((K, R)) * 1 / np.sqrt(K) * fk[:, None] * fr, "e4m3")
    w2p = pack_weight(n((K, R)) * 1 / np.sqrt(K) * fk[:, None] * fr, "e5m2")
    wbp = pack_weight(n((R, N)) * 1 / np.sqrt(R) / fr[:, None], "e2m1")
    sxp = pack_weight(n((L, O)) / fl[:, None], "e4m3")
    wsp = pack_weight(n((L, N)) * 1 / np.sqrt(L) * fl[:, None], "e4m3")
    return {
        "xt_words": xtp[0],
        "xt_scales": xtp[1],
        "w_words": wp[0],
        "w_scales": wp[1],
        "w2_words": w2p[0],
        "w2_scales": w2p[1],
        "wb_words": wbp[0],
        "wb_scales": wbp[1],
        "sx_words": sxp[0],
        "sx_scales": sxp[1],
        "ws_words": wsp[0],
        "ws_scales": wsp[1],
        "tz": (n((N, E))).astype(np.float32),
        "so": (np.random.uniform(0.6, 1.6, (N, 1))).astype(np.float32),
        "bo": (np.random.uniform(-1.0, 1.0, (N, 1))).astype(np.float32),
        "offs": striped(idx),
        "offs2": striped(idx2),
        "offs3": striped(idx3),
        "offs4": striped(idx4),
        "offs5": striped(idx5),
        "offs6": striped(idx6),
        "offs7": striped(idx7),
    }


def reference(xt_words, xt_scales, w_words, w_scales, w2_words, w2_scales, wb_words, wb_scales, sx_words, sx_scales, ws_words, ws_scales, tz, so, bo, offs, offs2, offs3, offs4, offs5, offs6, offs7):
    idx = unstriped(offs)
    idx2 = unstriped(offs2)
    idx3 = unstriped(offs3)
    idx4 = unstriped(offs4)
    idx5 = unstriped(offs5)
    idx6 = unstriped(offs6)
    idx7 = unstriped(offs7)
    xtu = unpack_weight(xt_words, xt_scales, "e2m1")
    wu = unpack_weight(w_words, w_scales, "e4m3")
    w2u = unpack_weight(w2_words, w2_scales, "e5m2")
    wbu = unpack_weight(wb_words, wb_scales, "e2m1")
    sxu = unpack_weight(sx_words, sx_scales, "e4m3")
    wsu = unpack_weight(ws_words, ws_scales, "e4m3")
    xtidxg = xtu[:, idx]
    a = wu.T @ xtidxg
    xtidx2g = xtu[:, idx2]
    b = w2u.T @ xtidx2g
    pw = np.zeros((R, C))
    pw[:, idx3] = a
    pv = np.zeros((R, C))
    pv[:, idx4] = b
    hid = np.maximum(pw[:, idx5], pv[:, idx6])
    hidq = mxq(hid, 0, "e5m2")
    p = wbu.T @ hidq + wsu.T @ sxu
    y = p * sigmoid(f64(tz)[:, idx7] * f64(so) + f64(bo))
    return y

from contextlib import ExitStack

import concourse.mybir as mybir

K, T, J, R, C, O, N, L, E = 512, 2048, 256, 512, 512, 256, 256, 512, 1024
FLOPS = 2 * (2 * K * R * J + R * N * O + L * N * O)

F32 = mybir.dt.float32
BF16 = mybir.dt.bfloat16
I32 = mybir.dt.int32
U32 = mybir.dt.uint32
U16 = mybir.dt.uint16
U8 = mybir.dt.uint8
E4M3 = mybir.dt.float8_e4m3fn_x4
E5M2 = mybir.dt.float8_e5m2_x4
E2M1 = mybir.dt.float4_e2m1fn_x4
ACT = mybir.ActivationFunctionType
ALU = mybir.AluOpType

P = 128
PACK = 4
HALF = 128


def tile_list_ahead_twoboards_skip_finalgate_kernel(
    tc, xt_words, xt_scales, w_words, w_scales, w2_words, w2_scales, wb_words, wb_scales,
    sx_words, sx_scales, ws_words, ws_scales, tz, so, bo,
    offs, offs2, offs3, offs4, offs5, offs6, offs7, out,
):
    nc = tc.nc
    with ExitStack() as ctx:
        lists = ctx.enter_context(tc.tile_pool(name="lists", bufs=1))
        sb = ctx.enter_context(tc.tile_pool(name="sb", bufs=1))
        ps = ctx.enter_context(tc.psum_pool(name="ps", bufs=1))

        def load_list(src, name):
            tile = lists.tile([P, J // 16], U16, name=name)
            nc.sync.dma_start(tile[:], src)
            return tile

        def load_words(src, width, dtype, name):
            tile = sb.tile([P, width], dtype, name=name, align_bytes=64)
            nc.sync.dma_start(tile[:].bitcast(I32), src.bitcast(I32))
            return tile

        def load_scale_rows(plane, src):
            for q in range(4):
                nc.sync.dma_start(plane[32 * q : 32 * q + 4, :].bitcast(I32), src[0, 4 * q : 4 * q + 4, :].bitcast(I32))

        def merged(words):
            return words[0].rearrange("p n t -> p (n t)")

        x_plane = sb.tile([P, T], U8, name="x_plane", align_bytes=64)
        nc.vector.memset(x_plane[:].bitcast(I32), 0)
        planes = sb.tile([P, 2 * R + 2 * N + O], U8, name="planes", align_bytes=64)
        nc.vector.memset(planes[:].bitcast(I32), 0)
        w_plane = planes[:, 0:R]
        w2_plane = planes[:, R : 2 * R]
        wb_plane = planes[:, 2 * R : 2 * R + N]
        ws_plane = planes[:, 2 * R + N : 2 * R + 2 * N]
        sx_plane = planes[:, 2 * R + 2 * N : 2 * R + 2 * N + O]

        boards = [[sb.tile([P, C], F32, name=f"board0_{t}") for t in range(PACK)]]
        for t in range(PACK):
            nc.vector.memset(boards[0][t][:], 0.0)

        pick1 = load_list(offs, "pick1")
        x_words = load_words(xt_words[0], T, U16, "x_words")
        load_scale_rows(x_plane, xt_scales)
        w_raw = load_words(merged(w_words), R, U32, "w_raw")
        load_scale_rows(w_plane, w_scales)
        pick2 = load_list(offs2, "pick2")
        put1 = load_list(offs3, "put1")
        w2_raw = load_words(merged(w2_words), R, U32, "w2_raw")
        load_scale_rows(w2_plane, w2_scales)
        read1 = load_list(offs5, "read1")
        put2 = load_list(offs4, "put2")
        read2 = load_list(offs6, "read2")
        ws_codes = load_words(merged(ws_words), N, U32, "ws_codes")
        sx_codes = load_words(merged(sx_words), O, U32, "sx_codes")
        load_scale_rows(ws_plane, ws_scales)
        load_scale_rows(sx_plane, sx_scales)
        wb_codes = load_words(wb_words[0], 2 * N, U8, "wb_codes")
        load_scale_rows(wb_plane, wb_scales)
        look = load_list(offs7, "look")
        slope = sb.tile([P, 2], F32, name="slope")
        offset = sb.tile([P, 2], F32, name="offset")
        with nc.allow_non_contiguous_dma(reason="one value a partition for each half of the output features"):
            nc.sync.dma_start(slope[:], so.rearrange("(h p) one -> p (h one)", p=P))
            nc.sync.dma_start(offset[:], bo.rearrange("(h p) one -> p (h one)", p=P))
        gate_table = []
        for h in range(2):
            rows = sb.tile([P, E], F32, name=f"gate_table{h}")
            nc.sync.dma_start(rows[:], tz[h * P : (h + 1) * P, :])
            gate_table.append(rows)

        def deal_words(raw, name, copy):
            dealt = sb.tile([P, R], U32, name=name, align_bytes=64)
            copy(
                dealt[:].rearrange("p (t c i) -> p c t i", t=PACK, i=4),
                raw[:].rearrange("p (c i t) -> p c t i", t=PACK, i=4),
            )
            return dealt

        def deal_bytes(plane, name, copy):
            dealt = sb.tile([P, R], U8, name=name, align_bytes=64)
            copy(
                dealt[:].rearrange("p (t c i) -> p c t i", t=PACK, i=16),
                plane.rearrange("p (c i t) -> p c t i", t=PACK, i=16),
            )
            return dealt

        def pick_tokens(pick, name):
            words = sb.tile([P, J], U16, name=name + "_words", align_bytes=64)
            plane = sb.tile([P, J], U8, name=name + "_plane", align_bytes=64)
            nc.vector.tensor_copy(words[:], x_words[:].indirect(pick[:]))
            nc.vector.tensor_copy(plane[:], x_plane[:].indirect(pick[:]))
            return words, plane

        def first_stage(s, codes, plane, fmt, tokens, put):
            for pair in range(2):
                acc = ps.tile([P, 2, J], F32, name=f"acc{s}_{pair}")
                for u in range(2):
                    cols = slice((2 * pair + u) * P, (2 * pair + u + 1) * P)
                    nc.tensor.matmul_mx(
                        out=acc[:, u, :],
                        lhsT=codes[:, cols].bitcast(fmt), lhsT_scale=plane[:, cols],
                        rhs=tokens[0][:].bitcast(E2M1), rhs_scale=tokens[1][:],
                        start=True, stop=True,
                    )
                sums = sb.tile([P, 2, J], F32, name=f"sums{s}_{pair}", align_bytes=64)
                nc.scalar.copy(sums[:], acc[:])
                nc.scalar.activation(boards[s][2 * pair][:].indirect(put[:]), sums[:, 0, :], ACT.Copy)
                nc.vector.tensor_copy(boards[s][2 * pair + 1][:].indirect(put[:]), sums[:, 1, :])

        def read_board(s, read, on_scalar):
            got = sb.tile([P, PACK, O], F32, name=f"got{s}")
            for t in range(PACK):
                window = boards[s][t][:].indirect(read[:])
                if t in on_scalar:
                    nc.scalar.activation(got[:, t, :], window, ACT.Copy)
                else:
                    nc.vector.tensor_copy(got[:, t, :], window)
            return got

        w_codes = deal_words(w_raw, "w_codes", nc.scalar.copy)
        tokens1 = pick_tokens(pick1, "tokens1")
        w_dealt = deal_bytes(w_plane, "w_dealt", nc.vector.tensor_copy)
        tokens2 = pick_tokens(pick2, "tokens2")
        first_stage(0, w_codes, w_dealt, E4M3, tokens1, put1)
        w2_codes = deal_words(w2_raw, "w2_codes", nc.gpsimd.tensor_copy)
        w2_dealt = deal_bytes(w2_plane, "w2_dealt", nc.gpsimd.tensor_copy)
        boards.append([])
        for t, spent in enumerate(("w_raw", "w_codes", "x_plane", "w2_raw")):
            board = sb.tile([P, C], F32, name=f"board1_{t}", tag=spent, align_bytes=64)
            nc.gpsimd.memset(board[:], 0.0)
            boards[1].append(board)
        got1 = read_board(0, read1, ())
        first_stage(1, w2_codes, w2_dealt, E5M2, tokens2, put2)
        got2 = read_board(1, read2, (0, 2))

        gate = sb.tile([P, 2, O], F32, name="gate")
        for h in range(2):
            nc.scalar.activation(
                gate[:, h, :], gate_table[h][:].indirect(look[:]), ACT.Sigmoid,
                bias=offset[:, h : h + 1], scale=slope[:, h : h + 1],
            )

        res_acc = [ps.tile([P, 2, HALF], F32, name=f"res_acc{g}") for g in range(2)]
        for g in range(2):
            reads = slice(g * HALF, (g + 1) * HALF)
            for h in range(2):
                feats = slice(h * P, (h + 1) * P)
                nc.tensor.matmul_mx(
                    out=res_acc[g][:, h, :],
                    lhsT=ws_codes[:, feats].bitcast(E4M3), lhsT_scale=ws_plane[:, feats],
                    rhs=sx_codes[:, reads].bitcast(E4M3), rhs_scale=sx_plane[:, reads],
                    start=(h == 0), stop=False,
                )

        hid = [sb.tile([P, HALF, PACK], BF16, name=f"hid{g}", align_bytes=64) for g in range(2)]
        hid_codes = [sb.tile([P, HALF], U32, name=f"hid_codes{g}", align_bytes=64) for g in range(2)]
        hid_plane = [sb.tile([P, HALF], U8, name=f"hid_plane{g}", align_bytes=64) for g in range(2)]
        for g in range(2):
            reads = slice(g * HALF, (g + 1) * HALF)
            nc.vector.tensor_tensor(
                hid[g][:].rearrange("p (c i) t -> p c t i", i=4),
                got1[:, :, reads].rearrange("p t (c i) -> p c t i", i=4),
                got2[:, :, reads].rearrange("p t (c i) -> p c t i", i=4),
                ALU.max,
            )
        for g in range(2):
            nc.vector.quantize_mx(
                out=hid_codes[g][:].bitcast(E5M2), scales=hid_plane[g][:],
                in_=hid[g][:].rearrange("p o t -> p (o t)"),
            )
            for h in range(2):
                nc.tensor.matmul_mx(
                    out=res_acc[g][:, h, :],
                    lhsT=wb_codes[:, 2 * h * P : 2 * (h + 1) * P].bitcast(E2M1),
                    lhsT_scale=wb_plane[:, h * P : (h + 1) * P],
                    rhs=hid_codes[g][:].bitcast(E5M2), rhs_scale=hid_plane[g][:],
                    start=False, stop=(h == 1),
                )
        out_view = out.rearrange("(h p) o -> p h o", p=P)
        for g in range(2):
            reads = slice(g * HALF, (g + 1) * HALF)
            result = sb.tile([P, 2, HALF], F32, name=f"result{g}")
            nc.vector.tensor_tensor(result[:], res_acc[g][:], gate[:, :, reads], ALU.mult)
            nc.sync.dma_start(out_view[:, :, reads], result[:])
